import numpy as np
import ml_dtypes


def mxq(x, axis, fmt="e4m3"):
    dtype, down = {"e4m3": (ml_dtypes.float8_e4m3fn, 7), "e5m2": (ml_dtypes.float8_e5m2, 14)}[fmt]
    v = np.moveaxis(np.asarray(x, np.float32).astype(ml_dtypes.bfloat16).astype(np.float64), axis, -1)
    blocks = v.reshape(v.shape[:-1] + (-1, 32))
    amax = np.abs(blocks).max(-1, keepdims=True)
    byte = np.maximum(np.where(amax > 0, np.frexp(amax)[1] - 1 + 127, 0) - down, 1)
    scale = np.exp2(byte - 127.0)
    codes = (blocks / scale).astype(np.float32).astype(dtype).astype(np.float64)
    return np.moveaxis((codes * scale).reshape(v.shape), -1, axis)


WIDE = False


def mx_kscale(k):
    if not WIDE:
        return np.ones(k)
    levels = np.array([10, -10, 5, -5, 0])
    if k % 512:
        return np.exp2(np.random.permutation(np.resize(levels, k // 32))).repeat(32)
    a = np.empty((k // 512, 16))
    for p in range(k // 512):
        a[p, :8] = np.random.permutation(np.resize(levels, 8))
        for g in range(8):
            far = levels[np.abs(levels - a[p, g]) >= 10]
            a[p, g + 8] = far[np.random.randint(len(far))]
    return np.exp2(a.ravel()).repeat(32)


def f64(x):
    return np.asarray(x).astype(np.float64)


E2M1 = np.array([0.0, 0.5, 1.0, 1.5, 2.0, 3.0, 4.0, 6.0, -0.0, -0.5, -1.0, -1.5, -2.0, -3.0, -4.0, -6.0])


def pack_weight(w, fmt):
    k, n = w.shape
    w = f64(np.asarray(w, np.float32).astype(ml_dtypes.bfloat16)).reshape(k // 32, 32, n)
    amax = np.abs(w).max(1)
    if fmt == "e4m3":
        byte = np.frexp(amax)[1] - 1 + 127 - 7
    else:
        mant, ex = np.frexp(amax / 6.0)
        byte = np.where(mant > 0.5, ex, ex - 1) + 127
    byte = np.clip(np.where(amax > 0, byte, 1), 1, 254)
    scaled = (w * np.exp2(127.0 - byte)[:, None, :]).reshape(k, n).astype(np.float32)
    by_word = np.ascontiguousarray(scaled.reshape(k // 512, 128, 4, n).transpose(0, 1, 3, 2))
    if fmt == "e4m3":
        words = by_word.astype(ml_dtypes.float8_e4m3fn).view(np.uint8)
    else:
        c = by_word.astype(ml_dtypes.float4_e2m1fn).view(np.uint8) & 0xF
        words = (c[..., 0::2] | (c[..., 1::2] << 4)).reshape(k // 512, 128, 2 * n)
    return np.ascontiguousarray(words), np.ascontiguousarray(byte.astype(np.uint8).reshape(k // 512, 16, n))


def unpack_weight(words, scales, fmt):
    g, _, n = scales.shape
    words = np.ascontiguousarray(words).reshape(g, 128, n, -1)
    if fmt == "e4m3":
        vals = words.view(ml_dtypes.float8_e4m3fn).astype(np.float64)
    else:
        nib = np.empty((g, 128, n, 4), np.uint8)
        nib[..., 0::2] = words & 0xF
        nib[..., 1::2] = words >> 4
        vals = E2M1[nib]
    vals = vals * np.repeat(np.exp2(scales.astype(np.float64) - 127.0), 8, axis=1)[..., None]
    return vals.transpose(0, 1, 3, 2).reshape(g * 512, n)


def planes(y):
    n, m = y.shape
    v = y.astype(np.float32).astype(ml_dtypes.bfloat16).astype(np.float64).reshape(n // 32, 32, m)
    top = np.abs(v).max(1)
    byte = np.clip(np.where(top > 0, np.frexp(top)[1] - 1 + 127 - 7, 1), 1, 254)
    codes = (v * np.exp2(127.0 - byte)[:, None, :]).reshape(n, m).astype(np.float32).astype(ml_dtypes.float8_e4m3fn).view(np.uint8)
    words = codes.reshape(n // 512, 128, 4, m).transpose(0, 1, 3, 2)
    return np.ascontiguousarray(words), np.ascontiguousarray(byte.astype(np.uint8).reshape(n // 512, 16, m))


K, M, T = 1536, 512, 1536


def setup_inputs():
    n = np.random.standard_normal
    s = mx_kscale(K)[:, None]
    p_w4 = pack_weight(n((K, M)) / np.sqrt(K) / s, "e2m1")
    p_w8 = pack_weight(n((K, M)) / np.sqrt(K) / s, "e4m3")
    return {
        "x": (n((K, T)) * s).astype(np.float32),
        "w4_words": p_w4[0],
        "w4_scales": p_w4[1],
        "w8_words": p_w8[0],
        "w8_scales": p_w8[1],
        "b": (0.3 * n(512)).astype(np.float32),
    }


def reference(x, w4_words, w4_scales, w8_words, w8_scales, b):
    xa_, xb_ = mxq(np.maximum(f64(x), 0.0), 0, "e4m3"), mxq(np.maximum(-f64(x), 0.0), 0, "e4m3")
    w4_ = unpack_weight(w4_words, w4_scales, "e2m1")
    w8_ = unpack_weight(w8_words, w8_scales, "e4m3")
    y = w4_.T @ xa_ + w8_.T @ xb_
    out_0 = y + f64(b)[:, None]
    return (out_0,) + planes(out_0)

@@ -1,0 +1,257 @@
+from contextlib import ExitStack
+
+import concourse.mybir as mybir
+
+K, M, T = 1536, 512, 1536
+FLOPS = 2 * 2 * K * M * T
+
+F32 = mybir.dt.float32
+BF16 = mybir.dt.bfloat16
+I32 = mybir.dt.int32
+U32 = mybir.dt.uint32
+U16 = mybir.dt.uint16
+U8 = mybir.dt.uint8
+FP8X4 = mybir.dt.float8_e4m3fn_x4
+FP4X4 = mybir.dt.float4_e2m1fn_x4
+ALU = mybir.AluOpType
+ACT = mybir.ActivationFunctionType
+
+P = 128
+PACK = 4
+K_PASS = P * PACK
+PASSES = K // K_PASS
+T_TILE = 512
+TILES = T // T_TILE
+RUN = 2
+W8_ROW = 4
+
+
+def interleaved(dst, src):
+    return (
+        dst.rearrange("p (c i j) -> p c j i", i=RUN, j=PACK),
+        src.rearrange("p j (c i) -> p c j i", i=RUN),
+    )
+
+
+def tile_mix_feat_fm_crelupl_bias_kernel(
+    tc, x, w4_words, w4_scales, w8_words, w8_scales, b, out_0, out_1, out_2
+):
+    nc = tc.nc
+    x_rows = x.rearrange("(a p j) t -> a p j t", p=P, j=PACK)
+    out_rows = out_0.rearrange("(p r) t -> p r t", r=PACK)
+    out_words = out_1[0].rearrange("p t i -> p (t i)").bitcast(I32)
+    out_scales = out_2[0].bitcast(I32)
+
+    pieces = []
+    for tt in range(TILES):
+        for a in range(PASSES):
+            if tt == 0 and a == 0:
+                pieces.extend([(tt, a, 0, 128), (tt, a, 128, 128), (tt, a, 256, 256)])
+            else:
+                pieces.append((tt, a, 0, T_TILE))
+
+    with ExitStack() as ctx:
+        keep = ctx.enter_context(tc.tile_pool(name="keep", bufs=1))
+        stage = ctx.enter_context(tc.tile_pool(name="stage", bufs=3))
+        psum = ctx.enter_context(tc.psum_pool(name="psum", bufs=2))
+        ctx.enter_context(tc.manual_schedule())
+
+        planes_raw = keep.tile([P, PASSES, M], U8, align_bytes=64)
+        planes = keep.tile([P, PASSES, M], U8, align_bytes=64)
+        w4_raw = keep.tile([P, PASSES, 2 * M], U8, align_bytes=64)
+        w4 = keep.tile([P, PASSES, 2 * M], U8, align_bytes=64)
+        w8_raw = keep.tile([P, PASSES, M], I32, align_bytes=64)
+        w8 = keep.tile([P, PASSES, M], I32, align_bytes=64)
+        bias = keep.tile([P, PACK], F32)
+        warm = keep.tile([P, 1], F32)
+        warm_out = keep.tile([P, 1], F32)
+        y_scales = keep.tile([P, T], U8, align_bytes=64)
+
+        nc.vector.memset(planes_raw[:].bitcast(I32), 0)
+        nc.vector.memset(warm[:], 0.0)
+        nc.scalar.activation(out=warm_out[:], in_=warm[:], func=ACT.Relu)
+
+        raws = []
+
+        def load_x(n):
+            tt, a, c0, w = pieces[n]
+            raw = keep.tile([P, PACK, w], F32, name="raw%d" % n)
+            t0 = tt * T_TILE + c0
+            nc.sync.dma_start(out=raw[:], in_=x_rows[a, :, :, t0 : t0 + w])
+            raws.append(raw)
+
+        def load_scales(scales, row):
+            by_r = scales.rearrange("a (q r) n -> r q a n", r=4)
+            for r in range(4):
+                nc.sync.dma_start(out=planes_raw[row + r : P : 32, :, :].bitcast(I32), in_=by_r[r].bitcast(I32))
+
+        load_x(0)
+        load_x(1)
+        load_scales(w8_scales, W8_ROW)
+        load_x(2)
+        nc.sync.dma_start(out=w8_raw[:], in_=w8_words.rearrange("a p n i -> p a (n i)").bitcast(I32))
+        load_scales(w4_scales, 0)
+        nc.sync.dma_start(out=w4_raw[:].bitcast(I32), in_=w4_words.rearrange("a p m -> p a m").bitcast(I32))
+        load_x(3)
+        nc.sync.dma_start(out=bias[:], in_=b.rearrange("(p r) -> p r", r=PACK))
+        for n in range(4, len(pieces)):
+            load_x(n)
+
+        codes = {}
+        for tt in range(TILES):
+            for a in range(PASSES):
+                for f in "ab":
+                    words = keep.tile([P, T_TILE], U32, name="words_%s%d%d" % (f, tt, a), align_bytes=64)
+                    scales = keep.tile([P, T_TILE], U8, name="scales_%s%d%d" % (f, tt, a), align_bytes=64)
+                    codes[f, tt, a] = (words, scales)
+
+        rounded = {}
+
+        def round_a(n):
+            w = pieces[n][3]
+            xa = stage.tile([P, PACK * w], BF16, name="xa", align_bytes=64)
+            dst, src = interleaved(xa[:], raws[n][:])
+            nc.scalar.activation(out=dst, in_=src, func=ACT.Relu)
+            rounded["a", n] = xa
+
+        def round_b(n):
+            w = pieces[n][3]
+            xb = stage.tile([P, PACK * w], BF16, name="xb", align_bytes=64)
+            dst, src = interleaved(xb[:], raws[n][:])
+            nc.vector.tensor_scalar(out=dst, in0=src, scalar1=-1.0, scalar2=0.0, op0=ALU.mult, op1=ALU.max)
+            rounded["b", n] = xb
+
+        def quantize(f, n):
+            tt, a, c0, w = pieces[n]
+            words, scales = codes[f, tt, a]
+            nc.vector.quantize_mx(
+                out=words[:, c0 : c0 + w].bitcast(FP8X4), scales=scales[:, c0 : c0 + w], in_=rounded[f, n][:]
+            )
+
+        def deal_w8():
+            nc.vector.tensor_copy(
+                out=w8[:].rearrange("p a (r m) -> p a m r", r=PACK), in_=w8_raw[:].rearrange("p a (m r) -> p a m r", r=PACK)
+            )
+
+        def deal_w4():
+            nc.vector.tensor_copy(
+                out=w4[:].bitcast(U16).rearrange("p a (r m) -> p a r m", r=PACK),
+                in_=w4_raw[:].bitcast(U16).rearrange("p a (m r) -> p a r m", r=PACK),
+            )
+
+        def deal_planes():
+            nc.vector.tensor_copy(
+                out=planes[:].rearrange("p a (r m) -> p a r m", r=PACK),
+                in_=planes_raw[:].rearrange("p a (m r) -> p a r m", r=PACK),
+            )
+
+        banks = {}
+
+        def multiply(f, tt, a):
+            words, scales = codes[f, tt, a]
+            for r in range(PACK):
+                first = f == "b" and a == 0
+                if first:
+                    banks[tt, r] = psum.tile([P, T_TILE], F32, name="acc%d" % r)
+                if f == "a":
+                    lhs = w4[:, a, 2 * P * r : 2 * P * (r + 1)].bitcast(FP4X4)
+                    lhs_scale = planes[:, a, P * r : P * (r + 1)]
+                else:
+                    lhs = w8[:, a, P * r : P * (r + 1)].bitcast(FP8X4)
+                    lhs_scale = planes[W8_ROW:P, a, P * r : P * (r + 1)]
+                nc.tensor.matmul_mx(
+                    out=banks[tt, r][:],
+                    lhsT=lhs,
+                    lhsT_scale=lhs_scale,
+                    rhs=words[:].bitcast(FP8X4),
+                    rhs_scale=scales[:],
+                    start=first,
+                    stop=(f == "a" and a == PASSES - 1),
+                )
+
+        results = {}
+
+        def add_bias(tt, r, engine):
+            if r == 0:
+                results[tt] = keep.tile([P, PACK, T_TILE], F32, name="y%d" % tt)
+            y = results[tt]
+            if engine == "scalar":
+                nc.scalar.activation(out=y[:, r, :], in_=banks[tt, r][:], func=ACT.Identity, bias=bias[:, r : r + 1])
+            else:
+                nc.vector.tensor_scalar(
+                    out=y[:, r, :], in0=banks[tt, r][:], scalar1=bias[:, r : r + 1], scalar2=None, op0=ALU.add
+                )
+
+        def store_y(tt, r0, r1):
+            cols = slice(tt * T_TILE, (tt + 1) * T_TILE)
+            nc.sync.dma_start(out=out_rows[:, r0:r1, cols], in_=results[tt][:, r0:r1, :])
+
+        y_rounded = {}
+
+        def round_y(tt):
+            yb = stage.tile([P, PACK * T_TILE], BF16, name="yb", bufs=2, align_bytes=64)
+            dst, src = interleaved(yb[:], results[tt][:])
+            nc.vector.tensor_copy(out=dst, in_=src)
+            y_rounded[tt] = yb
+
+        def quantize_y(tt):
+            cols = slice(tt * T_TILE, (tt + 1) * T_TILE)
+            y_words = keep.tile([P, T_TILE], U32, name="y_words%d" % tt, align_bytes=64)
+            nc.vector.quantize_mx(out=y_words[:].bitcast(FP8X4), scales=y_scales[:, cols], in_=y_rounded[tt][:])
+            nc.sync.dma_start(out=out_words[:, cols], in_=y_words[:].bitcast(I32))
+
+        last = len(pieces) - 1
+        pending = []
+
+        def ready(f, n):
+            tt, a, c0, w = pieces[n]
+            if c0 + w == T_TILE:
+                pending.append((f, tt, a))
+
+        def flush():
+            for f, tt, a in pending:
+                multiply(f, tt, a)
+            pending.clear()
+
+        for n in range(len(pieces)):
+            tt, a, c0, w = pieces[n]
+            round_a(n)
+            round_b(n)
+            if n > 0 and n != 3:
+                quantize("a", n - 1)
+                ready("a", n - 1)
+            if n == 3:
+                deal_w4()
+                ready("a", 2)
+            quantize("b", n)
+            ready("b", n)
+            if n == 2:
+                deal_w8()
+                quantize("a", 2)
+                deal_planes()
+            flush()
+            if (tt, a) == (1, 2):
+                for r in range(PACK):
+                    add_bias(0, r, "scalar")
+                store_y(0, 0, PACK)
+            if (tt, a) == (2, 0):
+                round_y(0)
+            if (tt, a) == (2, 1):
+                quantize_y(0)
+                for r in range(PACK):
+                    add_bias(1, r, "scalar")
+                store_y(1, 0, PACK)
+        round_y(1)
+        quantize("a", last)
+        ready("a", last)
+        flush()
+        quantize_y(1)
+        for r in range(PACK):
+            add_bias(2, r, "scalar" if r % 2 == 0 else "vector")
+            if r % 2 == 1:
+                store_y(2, r - 1, r + 1)
+        round_y(2)
+        quantize_y(2)
+        for q in range(4):
+            queue = nc.sync if q % 2 == 0 else nc.scalar
+            queue.dma_start(out=out_scales[4 * q : 4 * q + 4, :], in_=y_scales[32 * q : 32 * q + 4, :].bitcast(I32))

@@ -22,7 +22,7 @@ K_PASS = P * PACK
 PASSES = K // K_PASS
 T_TILE = 512
 TILES = T // T_TILE
-RUN = 2
+RUN = 4
 W8_ROW = 4
 
 
@@ -57,11 +57,11 @@ def tile_mix_feat_fm_crelupl_bias_kernel(
         ctx.enter_context(tc.manual_schedule())
 
         planes_raw = keep.tile([P, PASSES, M], U8, align_bytes=64)
-        planes = keep.tile([P, PASSES, M], U8, align_bytes=64)
+        planes = keep.tile([P, PACK, PASSES, P], U8, align_bytes=64)
         w4_raw = keep.tile([P, PASSES, 2 * M], U8, align_bytes=64)
-        w4 = keep.tile([P, PASSES, 2 * M], U8, align_bytes=64)
+        w4 = keep.tile([P, PACK, PASSES, 2 * P], U8, align_bytes=64)
         w8_raw = keep.tile([P, PASSES, M], I32, align_bytes=64)
-        w8 = keep.tile([P, PASSES, M], I32, align_bytes=64)
+        w8 = keep.tile([P, PACK, PASSES, P], I32, align_bytes=64)
         bias = keep.tile([P, PACK], F32)
         warm = keep.tile([P, 1], F32)
         warm_out = keep.tile([P, 1], F32)
@@ -130,19 +130,19 @@ def tile_mix_feat_fm_crelupl_bias_kernel(
 
         def deal_w8():
             nc.vector.tensor_copy(
-                out=w8[:].rearrange("p a (r m) -> p a m r", r=PACK), in_=w8_raw[:].rearrange("p a (m r) -> p a m r", r=PACK)
+                out=w8[:].rearrange("p r a m -> p (a m) r"), in_=w8_raw[:].rearrange("p a (m r) -> p (a m) r", r=PACK)
             )
 
         def deal_w4():
             nc.vector.tensor_copy(
-                out=w4[:].bitcast(U16).rearrange("p a (r m) -> p a r m", r=PACK),
-                in_=w4_raw[:].bitcast(U16).rearrange("p a (m r) -> p a r m", r=PACK),
+                out=w4[:].bitcast(U16).rearrange("p r a m -> p r (a m)"),
+                in_=w4_raw[:].bitcast(U16).rearrange("p a (m r) -> p r (a m)", r=PACK),
             )
 
         def deal_planes():
             nc.vector.tensor_copy(
-                out=planes[:].rearrange("p a (r m) -> p a r m", r=PACK),
-                in_=planes_raw[:].rearrange("p a (m r) -> p a r m", r=PACK),
+                out=planes[:].rearrange("p r a m -> p r (a m)"),
+                in_=planes_raw[:].rearrange("p a (m r) -> p r (a m)", r=PACK),
             )
 
         banks = {}
@@ -154,11 +154,11 @@ def tile_mix_feat_fm_crelupl_bias_kernel(
                 if first:
                     banks[tt, r] = psum.tile([P, T_TILE], F32, name="acc%d" % r)
                 if f == "a":
-                    lhs = w4[:, a, 2 * P * r : 2 * P * (r + 1)].bitcast(FP4X4)
-                    lhs_scale = planes[:, a, P * r : P * (r + 1)]
+                    lhs = w4[:, r, a, :].bitcast(FP4X4)
+                    lhs_scale = planes[:, r, a, :]
                 else:
-                    lhs = w8[:, a, P * r : P * (r + 1)].bitcast(FP8X4)
-                    lhs_scale = planes[W8_ROW:P, a, P * r : P * (r + 1)]
+                    lhs = w8[:, r, a, :].bitcast(FP8X4)
+                    lhs_scale = planes[W8_ROW:P, r, a, :]
                 nc.tensor.matmul_mx(
                     out=banks[tt, r][:],
                     lhsT=lhs,
@@ -200,6 +200,14 @@ def tile_mix_feat_fm_crelupl_bias_kernel(
             nc.vector.quantize_mx(out=y_words[:].bitcast(FP8X4), scales=y_scales[:, cols], in_=y_rounded[tt][:])
             nc.sync.dma_start(out=out_words[:, cols], in_=y_words[:].bitcast(I32))
 
+        def store_scales(t0, t1):
+            for q in range(4):
+                queue = nc.sync if q % 2 == 0 or t0 == 0 else nc.scalar
+                queue.dma_start(
+                    out=out_scales[4 * q : 4 * q + 4, t0 // 4 : t1 // 4],
+                    in_=y_scales[32 * q : 32 * q + 4, t0:t1].bitcast(I32),
+                )
+
         last = len(pieces) - 1
         pending = []
 
@@ -217,18 +225,15 @@ def tile_mix_feat_fm_crelupl_bias_kernel(
             tt, a, c0, w = pieces[n]
             round_a(n)
             round_b(n)
-            if n > 0 and n != 3:
+            if n > 0:
                 quantize("a", n - 1)
                 ready("a", n - 1)
-            if n == 3:
-                deal_w4()
-                ready("a", 2)
             quantize("b", n)
             ready("b", n)
             if n == 2:
                 deal_w8()
-                quantize("a", 2)
                 deal_planes()
+                deal_w4()
             flush()
             if (tt, a) == (1, 2):
                 for r in range(PACK):
@@ -246,12 +251,27 @@ def tile_mix_feat_fm_crelupl_bias_kernel(
         ready("a", last)
         flush()
         quantize_y(1)
+        store_scales(0, 2 * T_TILE)
         for r in range(PACK):
             add_bias(2, r, "scalar" if r % 2 == 0 else "vector")
             if r % 2 == 1:
                 store_y(2, r - 1, r + 1)
-        round_y(2)
-        quantize_y(2)
-        for q in range(4):
-            queue = nc.sync if q % 2 == 0 else nc.scalar
-            queue.dma_start(out=out_scales[4 * q : 4 * q + 4, :], in_=y_scales[32 * q : 32 * q + 4, :].bitcast(I32))
+        half = T_TILE // 2
+        y = results[2]
+        halves = []
+        for h in range(2):
+            yh = stage.tile([P, PACK * half], BF16, name="yh", bufs=2, align_bytes=64)
+            dst, src = interleaved(yh[:], y[:, :, h * half : (h + 1) * half])
+            if h == 0:
+                nc.vector.tensor_copy(out=dst, in_=src)
+            else:
+                split = 96 // RUN
+                nc.vector.tensor_copy(out=dst[:, :split], in_=src[:, :split])
+                nc.scalar.copy(out=dst[:, split:], in_=src[:, split:])
+            halves.append(yh)
+        for h in range(2):
+            cols = slice(2 * T_TILE + h * half, 2 * T_TILE + (h + 1) * half)
+            y_words = keep.tile([P, half], U32, name="y_last%d" % h, align_bytes=64)
+            nc.vector.quantize_mx(out=y_words[:].bitcast(FP8X4), scales=y_scales[:, cols], in_=halves[h][:])
+            nc.sync.dma_start(out=out_words[:, cols], in_=y_words[:].bitcast(I32))
+        store_scales(2 * T_TILE, T)

@@ -18,19 +18,16 @@ ACT = mybir.ActivationFunctionType
 
 P = 128
 PACK = 4
-K_PASS = P * PACK
-PASSES = K // K_PASS
+PAIR = 2
+PASSES = K // (P * PACK)
 T_TILE = 512
 TILES = T // T_TILE
-RUN = 4
+QUADRANT = 32
 W8_ROW = 4
-
-
-def interleaved(dst, src):
-    return (
-        dst.rearrange("p (c i j) -> p c j i", i=RUN, j=PACK),
-        src.rearrange("p j (c i) -> p c j i", i=RUN),
-    )
+RUN = 4
+FIRST_PARTS = (128, 128, 256)
+SCALAR_COLUMNS_MIDDLE = 128
+SCALAR_COLUMNS_LAST = 160
 
 
 def tile_mix_feat_fm_crelupl_bias_kernel(
@@ -42,13 +39,9 @@ def tile_mix_feat_fm_crelupl_bias_kernel(
     out_words = out_1[0].rearrange("p t i -> p (t i)").bitcast(I32)
     out_scales = out_2[0].bitcast(I32)
 
-    pieces = []
-    for tt in range(TILES):
-        for a in range(PASSES):
-            if tt == 0 and a == 0:
-                pieces.extend([(tt, a, 0, 128), (tt, a, 128, 128), (tt, a, 256, 256)])
-            else:
-                pieces.append((tt, a, 0, T_TILE))
+    pieces = [(0, 0, sum(FIRST_PARTS[:i]), width) for i, width in enumerate(FIRST_PARTS)]
+    pieces.extend((tile, a, 0, T_TILE) for tile in range(TILES) for a in range(PASSES) if (tile, a) != (0, 0))
+    first_whole = len(FIRST_PARTS)
 
     with ExitStack() as ctx:
         keep = ctx.enter_context(tc.tile_pool(name="keep", bufs=1))
@@ -63,215 +56,206 @@ def tile_mix_feat_fm_crelupl_bias_kernel(
         w8_raw = keep.tile([P, PASSES, M], I32, align_bytes=64)
         w8 = keep.tile([P, PACK, PASSES, P], I32, align_bytes=64)
         bias = keep.tile([P, PACK], F32)
-        warm = keep.tile([P, 1], F32)
-        warm_out = keep.tile([P, 1], F32)
         y_scales = keep.tile([P, T], U8, align_bytes=64)
 
         nc.vector.memset(planes_raw[:].bitcast(I32), 0)
+        warm = keep.tile([P, 1], F32)
+        warm_out = keep.tile([P, 1], F32)
         nc.vector.memset(warm[:], 0.0)
-        nc.scalar.activation(out=warm_out[:], in_=warm[:], func=ACT.Relu)
+        nc.scalar.activation(out=warm_out[:], in_=warm[:], func=ACT.Identity)
 
         raws = []
 
         def load_x(n):
-            tt, a, c0, w = pieces[n]
-            raw = keep.tile([P, PACK, w], F32, name="raw%d" % n)
-            t0 = tt * T_TILE + c0
-            nc.sync.dma_start(out=raw[:], in_=x_rows[a, :, :, t0 : t0 + w])
-            raws.append(raw)
+            tile, a, c0, width = pieces[n]
+            t0 = tile * T_TILE + c0
+            rows = PACK if n < first_whole else PAIR
+            parts = []
+            for j0 in range(0, PACK, rows):
+                raw = keep.tile([P, rows, width], F32, name="raw%d_%d" % (n, j0))
+                nc.sync.dma_start(out=raw[:], in_=x_rows[a, :, j0 : j0 + rows, t0 : t0 + width])
+                parts.append(raw)
+            raws.append(parts)
 
-        def load_scales(scales, row):
-            by_r = scales.rearrange("a (q r) n -> r q a n", r=4)
-            for r in range(4):
-                nc.sync.dma_start(out=planes_raw[row + r : P : 32, :, :].bitcast(I32), in_=by_r[r].bitcast(I32))
+        def load_scale_rows(rows):
+            for i in rows:
+                for scales, first in ((w8_scales, W8_ROW), (w4_scales, 0)):
+                    nc.sync.dma_start(
+                        out=planes_raw[first + i : P : QUADRANT, :, :].bitcast(I32),
+                        in_=scales.rearrange("a (q i) n -> i q a n", i=4)[i].bitcast(I32),
+                    )
 
         load_x(0)
         load_x(1)
-        load_scales(w8_scales, W8_ROW)
+        load_scale_rows((0, 1))
         load_x(2)
+        load_scale_rows((2, 3))
         nc.sync.dma_start(out=w8_raw[:], in_=w8_words.rearrange("a p n i -> p a (n i)").bitcast(I32))
-        load_scales(w4_scales, 0)
         nc.sync.dma_start(out=w4_raw[:].bitcast(I32), in_=w4_words.rearrange("a p m -> p a m").bitcast(I32))
-        load_x(3)
-        nc.sync.dma_start(out=bias[:], in_=b.rearrange("(p r) -> p r", r=PACK))
-        for n in range(4, len(pieces)):
+        for n in range(first_whole, len(pieces)):
             load_x(n)
+            if pieces[n][:2] == (1, 0):
+                nc.sync.dma_start(out=bias[:], in_=b.rearrange("(p r) -> p r", r=PACK))
 
-        codes = {}
-        for tt in range(TILES):
-            for a in range(PASSES):
-                for f in "ab":
-                    words = keep.tile([P, T_TILE], U32, name="words_%s%d%d" % (f, tt, a), align_bytes=64)
-                    scales = keep.tile([P, T_TILE], U8, name="scales_%s%d%d" % (f, tt, a), align_bytes=64)
-                    codes[f, tt, a] = (words, scales)
-
-        rounded = {}
-
-        def round_a(n):
-            w = pieces[n][3]
-            xa = stage.tile([P, PACK * w], BF16, name="xa", align_bytes=64)
-            dst, src = interleaved(xa[:], raws[n][:])
-            nc.scalar.activation(out=dst, in_=src, func=ACT.Relu)
-            rounded["a", n] = xa
-
-        def round_b(n):
-            w = pieces[n][3]
-            xb = stage.tile([P, PACK * w], BF16, name="xb", align_bytes=64)
-            dst, src = interleaved(xb[:], raws[n][:])
-            nc.vector.tensor_scalar(out=dst, in0=src, scalar1=-1.0, scalar2=0.0, op0=ALU.mult, op1=ALU.max)
-            rounded["b", n] = xb
-
-        def quantize(f, n):
-            tt, a, c0, w = pieces[n]
-            words, scales = codes[f, tt, a]
-            nc.vector.quantize_mx(
-                out=words[:, c0 : c0 + w].bitcast(FP8X4), scales=scales[:, c0 : c0 + w], in_=rounded[f, n][:]
-            )
-
-        def deal_w8():
+        def deal_weights():
             nc.vector.tensor_copy(
-                out=w8[:].rearrange("p r a m -> p (a m) r"), in_=w8_raw[:].rearrange("p a (m r) -> p (a m) r", r=PACK)
+                out=planes[:].rearrange("p r a m -> p r (a m)"),
+                in_=planes_raw[:].rearrange("p a (m r) -> p r (a m)", r=PACK),
             )
-
-        def deal_w4():
+            nc.vector.tensor_copy(
+                out=w8[:].rearrange("p r a m -> p (a m) r"),
+                in_=w8_raw[:].rearrange("p a (m r) -> p (a m) r", r=PACK),
+            )
             nc.vector.tensor_copy(
                 out=w4[:].bitcast(U16).rearrange("p r a m -> p r (a m)"),
                 in_=w4_raw[:].bitcast(U16).rearrange("p a (m r) -> p r (a m)", r=PACK),
             )
 
-        def deal_planes():
-            nc.vector.tensor_copy(
-                out=planes[:].rearrange("p r a m -> p r (a m)"),
-                in_=planes_raw[:].rearrange("p a (m r) -> p r (a m)", r=PACK),
+        def round_x(n):
+            width = pieces[n][3]
+            pairs = stage.tile([P, PACK * width], BF16, name="pairs", align_bytes=64)
+            rows = PACK // len(raws[n])
+            for i, raw in enumerate(raws[n]):
+                nc.scalar.copy(
+                    out=pairs[:, i * rows * width : (i + 1) * rows * width].rearrange(
+                        "p (h t e) -> p h t e", t=width, e=PAIR
+                    ),
+                    in_=raw[:].rearrange("p (h e) t -> p h t e", e=PAIR),
+                )
+            return pairs
+
+        def rectify(pairs, sign, name):
+            part = stage.tile(list(pairs.shape), BF16, name=name, bufs=2, align_bytes=64)
+            nc.vector.tensor_scalar(
+                out=part[:].rearrange("p (t h e) -> p t h e", h=PACK // PAIR, e=PAIR),
+                in0=pairs[:].rearrange("p (h t e) -> p t h e", h=PACK // PAIR, e=PAIR),
+                scalar1=sign,
+                scalar2=0.0,
+                op0=ALU.mult,
+                op1=ALU.max,
             )
+            return part
+
+        codes = {}
+
+        def quantize(feature, n, part):
+            tile, a, c0, width = pieces[n]
+            if c0 == 0:
+                label = "%s%d%d" % (feature, tile, a)
+                words = keep.tile([P, T_TILE], U32, name="words_" + label, align_bytes=64)
+                scales = keep.tile([P, T_TILE], U8, name="scales_" + label, align_bytes=64)
+                codes[feature, tile, a] = (words, scales)
+            words, scales = codes[feature, tile, a]
+            cols = slice(c0, c0 + width)
+            nc.vector.quantize_mx(out=words[:, cols].bitcast(FP8X4), scales=scales[:, cols], in_=part[:])
 
         banks = {}
 
-        def multiply(f, tt, a):
-            words, scales = codes[f, tt, a]
-            for r in range(PACK):
-                first = f == "b" and a == 0
-                if first:
-                    banks[tt, r] = psum.tile([P, T_TILE], F32, name="acc%d" % r)
-                if f == "a":
-                    lhs = w4[:, r, a, :].bitcast(FP4X4)
-                    lhs_scale = planes[:, r, a, :]
-                else:
-                    lhs = w8[:, r, a, :].bitcast(FP8X4)
-                    lhs_scale = planes[W8_ROW:P, r, a, :]
-                nc.tensor.matmul_mx(
-                    out=banks[tt, r][:],
-                    lhsT=lhs,
-                    lhsT_scale=lhs_scale,
-                    rhs=words[:].bitcast(FP8X4),
-                    rhs_scale=scales[:],
-                    start=first,
-                    stop=(f == "a" and a == PASSES - 1),
-                )
-
-        results = {}
-
-        def add_bias(tt, r, engine):
-            if r == 0:
-                results[tt] = keep.tile([P, PACK, T_TILE], F32, name="y%d" % tt)
-            y = results[tt]
-            if engine == "scalar":
-                nc.scalar.activation(out=y[:, r, :], in_=banks[tt, r][:], func=ACT.Identity, bias=bias[:, r : r + 1])
-            else:
-                nc.vector.tensor_scalar(
-                    out=y[:, r, :], in0=banks[tt, r][:], scalar1=bias[:, r : r + 1], scalar2=None, op0=ALU.add
-                )
-
-        def store_y(tt, r0, r1):
-            cols = slice(tt * T_TILE, (tt + 1) * T_TILE)
-            nc.sync.dma_start(out=out_rows[:, r0:r1, cols], in_=results[tt][:, r0:r1, :])
-
-        y_rounded = {}
-
-        def round_y(tt):
-            yb = stage.tile([P, PACK * T_TILE], BF16, name="yb", bufs=2, align_bytes=64)
-            dst, src = interleaved(yb[:], results[tt][:])
-            nc.vector.tensor_copy(out=dst, in_=src)
-            y_rounded[tt] = yb
-
-        def quantize_y(tt):
-            cols = slice(tt * T_TILE, (tt + 1) * T_TILE)
-            y_words = keep.tile([P, T_TILE], U32, name="y_words%d" % tt, align_bytes=64)
-            nc.vector.quantize_mx(out=y_words[:].bitcast(FP8X4), scales=y_scales[:, cols], in_=y_rounded[tt][:])
-            nc.sync.dma_start(out=out_words[:, cols], in_=y_words[:].bitcast(I32))
-
-        def store_scales(t0, t1):
-            for q in range(4):
-                queue = nc.sync if q % 2 == 0 or t0 == 0 else nc.scalar
-                queue.dma_start(
-                    out=out_scales[4 * q : 4 * q + 4, t0 // 4 : t1 // 4],
-                    in_=y_scales[32 * q : 32 * q + 4, t0:t1].bitcast(I32),
-                )
-
-        last = len(pieces) - 1
-        pending = []
-
-        def ready(f, n):
-            tt, a, c0, w = pieces[n]
-            if c0 + w == T_TILE:
-                pending.append((f, tt, a))
-
-        def flush():
-            for f, tt, a in pending:
-                multiply(f, tt, a)
-            pending.clear()
-
-        for n in range(len(pieces)):
-            tt, a, c0, w = pieces[n]
-            round_a(n)
-            round_b(n)
-            if n > 0:
-                quantize("a", n - 1)
-                ready("a", n - 1)
-            quantize("b", n)
-            ready("b", n)
-            if n == 2:
-                deal_w8()
-                deal_planes()
-                deal_w4()
-            flush()
-            if (tt, a) == (1, 2):
+        def multiply(tile, a):
+            for feature in "ba":
+                words, scales = codes[feature, tile, a]
+                first = a == 0 and feature == "b"
                 for r in range(PACK):
-                    add_bias(0, r, "scalar")
-                store_y(0, 0, PACK)
-            if (tt, a) == (2, 0):
-                round_y(0)
-            if (tt, a) == (2, 1):
-                quantize_y(0)
-                for r in range(PACK):
-                    add_bias(1, r, "scalar")
-                store_y(1, 0, PACK)
-        round_y(1)
-        quantize("a", last)
-        ready("a", last)
-        flush()
-        quantize_y(1)
-        store_scales(0, 2 * T_TILE)
-        for r in range(PACK):
-            add_bias(2, r, "scalar" if r % 2 == 0 else "vector")
-            if r % 2 == 1:
-                store_y(2, r - 1, r + 1)
-        half = T_TILE // 2
-        y = results[2]
-        halves = []
-        for h in range(2):
-            yh = stage.tile([P, PACK * half], BF16, name="yh", bufs=2, align_bytes=64)
-            dst, src = interleaved(yh[:], y[:, :, h * half : (h + 1) * half])
-            if h == 0:
-                nc.vector.tensor_copy(out=dst, in_=src)
-            else:
-                split = 96 // RUN
+                    if first:
+                        banks[tile, r] = psum.tile([P, T_TILE], F32, name="acc%d" % r)
+                    if feature == "a":
+                        weights, weight_scales = w4[:, r, a, :].bitcast(FP4X4), planes[:, r, a, :]
+                    else:
+                        weights, weight_scales = w8[:, r, a, :].bitcast(FP8X4), planes[W8_ROW:P, r, a, :]
+                    nc.tensor.matmul_mx(
+                        out=banks[tile, r][:],
+                        lhsT=weights,
+                        lhsT_scale=weight_scales,
+                        rhs=words[:].bitcast(FP8X4),
+                        rhs_scale=scales[:],
+                        start=first,
+                        stop=(a == PASSES - 1 and feature == "a"),
+                    )
+
+        results = [keep.tile([P, PACK, T_TILE], F32, name="y%d" % tile) for tile in range(TILES)]
+
+        def add_bias_scalar(tile, r):
+            nc.scalar.activation(
+                out=results[tile][:, r, :], in_=banks[tile, r][:], func=ACT.Identity, bias=bias[:, r : r + 1]
+            )
+
+        def add_bias_vector(tile, r):
+            nc.vector.tensor_scalar(
+                out=results[tile][:, r, :],
+                in0=banks[tile, r][:],
+                scalar1=bias[:, r : r + 1],
+                scalar2=None,
+                op0=ALU.add,
+            )
+
+        def store_y(tile, r0, r1):
+            cols = slice(tile * T_TILE, (tile + 1) * T_TILE)
+            nc.sync.dma_start(out=out_rows[:, r0:r1, cols], in_=results[tile][:, r0:r1, :])
+
+        def round_y(tile, c0, width, scalar_columns, name):
+            rounded = stage.tile([P, PACK * width], BF16, name=name, bufs=2, align_bytes=64)
+            dst = rounded[:].rearrange("p (c i r) -> p c r i", i=RUN, r=PACK)
+            src = results[tile][:, :, c0 : c0 + width].rearrange("p r (c i) -> p c r i", i=RUN)
+            split = (width - scalar_columns) // RUN
+            if split > 0:
                 nc.vector.tensor_copy(out=dst[:, :split], in_=src[:, :split])
+            if scalar_columns > 0:
                 nc.scalar.copy(out=dst[:, split:], in_=src[:, split:])
-            halves.append(yh)
+            return rounded
+
+        y_words = [keep.tile([P, T_TILE], U32, name="y_words%d" % tile, align_bytes=64) for tile in range(TILES)]
+
+        def quantize_y(tile, c0, rounded):
+            width = rounded.shape[1] // PACK
+            t0 = tile * T_TILE + c0
+            nc.vector.quantize_mx(
+                out=y_words[tile][:, c0 : c0 + width].bitcast(FP8X4), scales=y_scales[:, t0 : t0 + width], in_=rounded[:]
+            )
+
+        def store_words(tile):
+            nc.sync.dma_start(out=out_words[:, tile * T_TILE : (tile + 1) * T_TILE], in_=y_words[tile][:].bitcast(I32))
+
+        for n, (tile, a, c0, width) in enumerate(pieces):
+            pairs = round_x(n)
+            xb = rectify(pairs, -1.0, "xb")
+            xa = rectify(pairs, 1.0, "xa")
+            quantize("b", n, xb)
+            quantize("a", n, xa)
+            if n == first_whole - 1:
+                deal_weights()
+            if c0 + width == T_TILE:
+                multiply(tile, a)
+            if (tile, a) == (1, 1):
+                for r in range(PACK // 2):
+                    add_bias_scalar(0, r)
+                store_y(0, 0, PACK // 2)
+                for r in range(PACK // 2, PACK):
+                    add_bias_vector(0, r)
+                store_y(0, PACK // 2, PACK)
+
+        for r in range(PACK):
+            add_bias_scalar(1, r)
+        store_y(1, 0, PACK)
+        rounded_first = round_y(0, 0, T_TILE, T_TILE, "y_rounded")
+        rounded_middle = round_y(1, 0, T_TILE, SCALAR_COLUMNS_MIDDLE, "y_rounded")
+        quantize_y(0, 0, rounded_first)
+        store_words(0)
+        quantize_y(1, 0, rounded_middle)
+        store_words(1)
+
+        last = TILES - 1
+        for r in range(PACK - 1):
+            add_bias_scalar(last, r)
+            store_y(last, r, r + 1)
+        add_bias_vector(last, PACK - 1)
+        store_y(last, PACK - 1, PACK)
+        half = T_TILE // 2
+        rounded_halves = [round_y(last, 0, half, 0, "y_half"), round_y(last, half, half, SCALAR_COLUMNS_LAST, "y_half")]
         for h in range(2):
-            cols = slice(2 * T_TILE + h * half, 2 * T_TILE + (h + 1) * half)
-            y_words = keep.tile([P, half], U32, name="y_last%d" % h, align_bytes=64)
-            nc.vector.quantize_mx(out=y_words[:].bitcast(FP8X4), scales=y_scales[:, cols], in_=halves[h][:])
-            nc.sync.dma_start(out=out_words[:, cols], in_=y_words[:].bitcast(I32))
-        store_scales(2 * T_TILE, T)
+            quantize_y(last, h * half, rounded_halves[h])
+        store_words(last)
+        for q in range(P // QUADRANT):
+            queue = nc.scalar if q % 2 == 0 else nc.sync
+            queue.dma_start(
+                out=out_scales[4 * q : 4 * q + 4, :], in_=y_scales[QUADRANT * q : QUADRANT * q + 4, :].bitcast(I32)
+            )

@@ -18,16 +18,22 @@ ACT = mybir.ActivationFunctionType
 
 P = 128
 PACK = 4
-PAIR = 2
 PASSES = K // (P * PACK)
 T_TILE = 512
 TILES = T // T_TILE
 QUADRANT = 32
-W8_ROW = 4
+SCALE_ROWS = 4
+W8_FIRST = 4
 RUN = 4
-FIRST_PARTS = (128, 128, 256)
-SCALAR_COLUMNS_MIDDLE = 128
+SCALAR_COLUMNS_MIDDLE = 256
 SCALAR_COLUMNS_LAST = 160
+
+
+def interleaved(dst, src):
+    return (
+        dst.rearrange("p (c i j) -> p c j i", i=RUN, j=PACK),
+        src.rearrange("p j (c i) -> p c j i", i=RUN),
+    )
 
 
 def tile_mix_feat_fm_crelupl_bias_kernel(
@@ -38,14 +44,12 @@ def tile_mix_feat_fm_crelupl_bias_kernel(
     out_rows = out_0.rearrange("(p r) t -> p r t", r=PACK)
     out_words = out_1[0].rearrange("p t i -> p (t i)").bitcast(I32)
     out_scales = out_2[0].bitcast(I32)
-
-    pieces = [(0, 0, sum(FIRST_PARTS[:i]), width) for i, width in enumerate(FIRST_PARTS)]
-    pieces.extend((tile, a, 0, T_TILE) for tile in range(TILES) for a in range(PASSES) if (tile, a) != (0, 0))
-    first_whole = len(FIRST_PARTS)
+    chunks = [(tile, a) for tile in range(TILES) for a in range(PASSES)]
+    first_tile, middle_tile, last_tile = range(TILES)
 
     with ExitStack() as ctx:
         keep = ctx.enter_context(tc.tile_pool(name="keep", bufs=1))
-        stage = ctx.enter_context(tc.tile_pool(name="stage", bufs=3))
+        stage = ctx.enter_context(tc.tile_pool(name="stage", bufs=2))
         psum = ctx.enter_context(tc.psum_pool(name="psum", bufs=2))
         ctx.enter_context(tc.manual_schedule())
 
@@ -56,206 +60,162 @@ def tile_mix_feat_fm_crelupl_bias_kernel(
         w8_raw = keep.tile([P, PASSES, M], I32, align_bytes=64)
         w8 = keep.tile([P, PACK, PASSES, P], I32, align_bytes=64)
         bias = keep.tile([P, PACK], F32)
-        y_scales = keep.tile([P, T], U8, align_bytes=64)
 
         nc.vector.memset(planes_raw[:].bitcast(I32), 0)
-        warm = keep.tile([P, 1], F32)
+        warm_in = keep.tile([P, 1], F32)
         warm_out = keep.tile([P, 1], F32)
-        nc.vector.memset(warm[:], 0.0)
-        nc.scalar.activation(out=warm_out[:], in_=warm[:], func=ACT.Identity)
-
-        raws = []
-
-        def load_x(n):
-            tile, a, c0, width = pieces[n]
-            t0 = tile * T_TILE + c0
-            rows = PACK if n < first_whole else PAIR
-            parts = []
-            for j0 in range(0, PACK, rows):
-                raw = keep.tile([P, rows, width], F32, name="raw%d_%d" % (n, j0))
-                nc.sync.dma_start(out=raw[:], in_=x_rows[a, :, j0 : j0 + rows, t0 : t0 + width])
-                parts.append(raw)
-            raws.append(parts)
+        nc.vector.memset(warm_in[:], 0.0)
+        nc.scalar.activation(out=warm_out[:], in_=warm_in[:], func=ACT.Relu)
 
         def load_scale_rows(rows):
             for i in rows:
-                for scales, first in ((w8_scales, W8_ROW), (w4_scales, 0)):
+                for scales, first in ((w8_scales, W8_FIRST), (w4_scales, 0)):
                     nc.sync.dma_start(
                         out=planes_raw[first + i : P : QUADRANT, :, :].bitcast(I32),
-                        in_=scales.rearrange("a (q i) n -> i q a n", i=4)[i].bitcast(I32),
+                        in_=scales.rearrange("a (q i) n -> i q a n", i=SCALE_ROWS)[i].bitcast(I32),
                     )
 
-        load_x(0)
-        load_x(1)
-        load_scale_rows((0, 1))
-        load_x(2)
-        load_scale_rows((2, 3))
-        nc.sync.dma_start(out=w8_raw[:], in_=w8_words.rearrange("a p n i -> p a (n i)").bitcast(I32))
         nc.sync.dma_start(out=w4_raw[:].bitcast(I32), in_=w4_words.rearrange("a p m -> p a m").bitcast(I32))
-        for n in range(first_whole, len(pieces)):
-            load_x(n)
-            if pieces[n][:2] == (1, 0):
+        load_scale_rows(range(SCALE_ROWS // 2))
+        nc.sync.dma_start(out=w8_raw[:], in_=w8_words.rearrange("a p n i -> p a (n i)").bitcast(I32))
+        load_scale_rows(range(SCALE_ROWS // 2, SCALE_ROWS))
+        raws = {}
+        for tile, a in chunks:
+            raw = keep.tile([P, PACK, T_TILE], F32, name="raw%d%d" % (tile, a))
+            nc.sync.dma_start(out=raw[:], in_=x_rows[a, :, :, tile * T_TILE : (tile + 1) * T_TILE])
+            raws[tile, a] = raw
+            if (tile, a) == (middle_tile, 0):
                 nc.sync.dma_start(out=bias[:], in_=b.rearrange("(p r) -> p r", r=PACK))
 
-        def deal_weights():
-            nc.vector.tensor_copy(
-                out=planes[:].rearrange("p r a m -> p r (a m)"),
-                in_=planes_raw[:].rearrange("p a (m r) -> p r (a m)", r=PACK),
-            )
-            nc.vector.tensor_copy(
-                out=w8[:].rearrange("p r a m -> p (a m) r"),
-                in_=w8_raw[:].rearrange("p a (m r) -> p (a m) r", r=PACK),
-            )
-            nc.vector.tensor_copy(
-                out=w4[:].bitcast(U16).rearrange("p r a m -> p r (a m)"),
-                in_=w4_raw[:].bitcast(U16).rearrange("p a (m r) -> p r (a m)", r=PACK),
-            )
+        nc.vector.tensor_copy(
+            out=w4[:].bitcast(U16).rearrange("p r a m -> p r (a m)"),
+            in_=w4_raw[:].bitcast(U16).rearrange("p a (m r) -> p r (a m)", r=PACK),
+        )
+        nc.vector.tensor_copy(
+            out=w8[:].rearrange("p r a (c i) -> p (a c) r i", i=RUN),
+            in_=w8_raw[:].rearrange("p a (c i r) -> p (a c) r i", i=RUN, r=PACK),
+        )
+        nc.vector.tensor_copy(
+            out=planes[:].rearrange("p r a m -> p r (a m)"),
+            in_=planes_raw[:].rearrange("p a (m r) -> p r (a m)", r=PACK),
+        )
 
-        def round_x(n):
-            width = pieces[n][3]
-            pairs = stage.tile([P, PACK * width], BF16, name="pairs", align_bytes=64)
-            rows = PACK // len(raws[n])
-            for i, raw in enumerate(raws[n]):
-                nc.scalar.copy(
-                    out=pairs[:, i * rows * width : (i + 1) * rows * width].rearrange(
-                        "p (h t e) -> p h t e", t=width, e=PAIR
-                    ),
-                    in_=raw[:].rearrange("p (h e) t -> p h t e", e=PAIR),
-                )
-            return pairs
+        def positive_part(chunk):
+            xa = stage.tile([P, PACK * T_TILE], BF16, name="xa", bufs=3, align_bytes=64)
+            dst, src = interleaved(xa[:], raws[chunk][:])
+            nc.scalar.activation(out=dst, in_=src, func=ACT.Relu)
+            return xa
 
-        def rectify(pairs, sign, name):
-            part = stage.tile(list(pairs.shape), BF16, name=name, bufs=2, align_bytes=64)
-            nc.vector.tensor_scalar(
-                out=part[:].rearrange("p (t h e) -> p t h e", h=PACK // PAIR, e=PAIR),
-                in0=pairs[:].rearrange("p (h t e) -> p t h e", h=PACK // PAIR, e=PAIR),
-                scalar1=sign,
-                scalar2=0.0,
-                op0=ALU.mult,
-                op1=ALU.max,
-            )
-            return part
-
-        codes = {}
-
-        def quantize(feature, n, part):
-            tile, a, c0, width = pieces[n]
-            if c0 == 0:
-                label = "%s%d%d" % (feature, tile, a)
-                words = keep.tile([P, T_TILE], U32, name="words_" + label, align_bytes=64)
-                scales = keep.tile([P, T_TILE], U8, name="scales_" + label, align_bytes=64)
-                codes[feature, tile, a] = (words, scales)
-            words, scales = codes[feature, tile, a]
-            cols = slice(c0, c0 + width)
-            nc.vector.quantize_mx(out=words[:, cols].bitcast(FP8X4), scales=scales[:, cols], in_=part[:])
+        def negative_part(chunk):
+            xb = stage.tile([P, PACK * T_TILE], BF16, name="xb", align_bytes=64)
+            dst, src = interleaved(xb[:], raws[chunk][:])
+            nc.vector.tensor_scalar(out=dst, in0=src, scalar1=-1.0, scalar2=0.0, op0=ALU.mult, op1=ALU.max)
+            return xb
 
         banks = {}
 
-        def multiply(tile, a):
-            for feature in "ba":
-                words, scales = codes[feature, tile, a]
-                first = a == 0 and feature == "b"
-                for r in range(PACK):
-                    if first:
-                        banks[tile, r] = psum.tile([P, T_TILE], F32, name="acc%d" % r)
-                    if feature == "a":
-                        weights, weight_scales = w4[:, r, a, :].bitcast(FP4X4), planes[:, r, a, :]
-                    else:
-                        weights, weight_scales = w8[:, r, a, :].bitcast(FP8X4), planes[W8_ROW:P, r, a, :]
-                    nc.tensor.matmul_mx(
-                        out=banks[tile, r][:],
-                        lhsT=weights,
-                        lhsT_scale=weight_scales,
-                        rhs=words[:].bitcast(FP8X4),
-                        rhs_scale=scales[:],
-                        start=first,
-                        stop=(a == PASSES - 1 and feature == "a"),
-                    )
+        def quantize_and_multiply(feature, chunk, part):
+            tile, a = chunk
+            label = "%s%d%d" % (feature, tile, a)
+            words = keep.tile([P, T_TILE], U32, name="words_" + label, align_bytes=64)
+            scales = keep.tile([P, T_TILE], U8, name="scales_" + label, align_bytes=64)
+            nc.vector.quantize_mx(out=words[:].bitcast(FP8X4), scales=scales[:], in_=part[:])
+            opens = feature == "b" and a == 0
+            closes = feature == "a" and a == PASSES - 1
+            for r in range(PACK):
+                if opens:
+                    banks[tile, r] = psum.tile([P, T_TILE], F32, name="acc%d" % r)
+                if feature == "a":
+                    weights, weight_scales = w4[:, r, a, :].bitcast(FP4X4), planes[:, r, a, :]
+                else:
+                    weights, weight_scales = w8[:, r, a, :].bitcast(FP8X4), planes[W8_FIRST:P, r, a, :]
+                nc.tensor.matmul_mx(
+                    out=banks[tile, r][:],
+                    lhsT=weights,
+                    lhsT_scale=weight_scales,
+                    rhs=words[:].bitcast(FP8X4),
+                    rhs_scale=scales[:],
+                    start=opens,
+                    stop=closes,
+                )
 
         results = [keep.tile([P, PACK, T_TILE], F32, name="y%d" % tile) for tile in range(TILES)]
+        y_words = keep.tile([P, T], U32, align_bytes=64)
+        y_scales = keep.tile([P, T], U8, align_bytes=64)
 
-        def add_bias_scalar(tile, r):
+        def add_bias_on_scalar(tile, r):
             nc.scalar.activation(
                 out=results[tile][:, r, :], in_=banks[tile, r][:], func=ACT.Identity, bias=bias[:, r : r + 1]
             )
 
-        def add_bias_vector(tile, r):
+        def add_bias_on_vector(tile, r):
             nc.vector.tensor_scalar(
-                out=results[tile][:, r, :],
-                in0=banks[tile, r][:],
-                scalar1=bias[:, r : r + 1],
-                scalar2=None,
-                op0=ALU.add,
+                out=results[tile][:, r, :], in0=banks[tile, r][:], scalar1=bias[:, r : r + 1], scalar2=None, op0=ALU.add
             )
 
-        def store_y(tile, r0, r1):
+        def store_result(tile, r0, r1):
             cols = slice(tile * T_TILE, (tile + 1) * T_TILE)
             nc.sync.dma_start(out=out_rows[:, r0:r1, cols], in_=results[tile][:, r0:r1, :])
 
-        def round_y(tile, c0, width, scalar_columns, name):
-            rounded = stage.tile([P, PACK * width], BF16, name=name, bufs=2, align_bytes=64)
-            dst = rounded[:].rearrange("p (c i r) -> p c r i", i=RUN, r=PACK)
-            src = results[tile][:, :, c0 : c0 + width].rearrange("p r (c i) -> p c r i", i=RUN)
+        def round_result(tile, c0, width, scalar_columns):
+            rounded = keep.tile([P, PACK * width], BF16, name="rounded%d_%d" % (tile, c0), align_bytes=64)
+            dst, src = interleaved(rounded[:], results[tile][:, :, c0 : c0 + width])
             split = (width - scalar_columns) // RUN
-            if split > 0:
-                nc.vector.tensor_copy(out=dst[:, :split], in_=src[:, :split])
+            nc.vector.tensor_copy(out=dst[:, :split], in_=src[:, :split])
             if scalar_columns > 0:
                 nc.scalar.copy(out=dst[:, split:], in_=src[:, split:])
             return rounded
 
-        y_words = [keep.tile([P, T_TILE], U32, name="y_words%d" % tile, align_bytes=64) for tile in range(TILES)]
-
-        def quantize_y(tile, c0, rounded):
-            width = rounded.shape[1] // PACK
-            t0 = tile * T_TILE + c0
-            nc.vector.quantize_mx(
-                out=y_words[tile][:, c0 : c0 + width].bitcast(FP8X4), scales=y_scales[:, t0 : t0 + width], in_=rounded[:]
-            )
+        def quantize_result(tile, c0, width, rounded):
+            cols = slice(tile * T_TILE + c0, tile * T_TILE + c0 + width)
+            nc.vector.quantize_mx(out=y_words[:, cols].bitcast(FP8X4), scales=y_scales[:, cols], in_=rounded[:])
 
         def store_words(tile):
-            nc.sync.dma_start(out=out_words[:, tile * T_TILE : (tile + 1) * T_TILE], in_=y_words[tile][:].bitcast(I32))
+            cols = slice(tile * T_TILE, (tile + 1) * T_TILE)
+            nc.sync.dma_start(out=out_words[:, cols], in_=y_words[:, cols].bitcast(I32))
 
-        for n, (tile, a, c0, width) in enumerate(pieces):
-            pairs = round_x(n)
-            xb = rectify(pairs, -1.0, "xb")
-            xa = rectify(pairs, 1.0, "xa")
-            quantize("b", n, xb)
-            quantize("a", n, xa)
-            if n == first_whole - 1:
-                deal_weights()
-            if c0 + width == T_TILE:
-                multiply(tile, a)
-            if (tile, a) == (1, 1):
-                for r in range(PACK // 2):
-                    add_bias_scalar(0, r)
-                store_y(0, 0, PACK // 2)
-                for r in range(PACK // 2, PACK):
-                    add_bias_vector(0, r)
-                store_y(0, PACK // 2, PACK)
+        last_bank = PACK - 1
+        xa_before = None
+        for step, chunk in enumerate(chunks):
+            xa = positive_part(chunk)
+            xb = negative_part(chunk)
+            if step > 0:
+                quantize_and_multiply("a", chunks[step - 1], xa_before)
+            quantize_and_multiply("b", chunk, xb)
+            xa_before = xa
+            if chunk == (middle_tile, 1):
+                for r in range(last_bank):
+                    add_bias_on_scalar(first_tile, r)
+                add_bias_on_vector(first_tile, last_bank)
+                store_result(first_tile, 0, PACK)
+            if chunk == (last_tile, 1):
+                add_bias_on_vector(middle_tile, last_bank)
 
-        for r in range(PACK):
-            add_bias_scalar(1, r)
-        store_y(1, 0, PACK)
-        rounded_first = round_y(0, 0, T_TILE, T_TILE, "y_rounded")
-        rounded_middle = round_y(1, 0, T_TILE, SCALAR_COLUMNS_MIDDLE, "y_rounded")
-        quantize_y(0, 0, rounded_first)
-        store_words(0)
-        quantize_y(1, 0, rounded_middle)
-        store_words(1)
+        for r in range(last_bank):
+            add_bias_on_scalar(middle_tile, r)
+        store_result(middle_tile, 0, PACK)
+        rounded_first = round_result(first_tile, 0, T_TILE, 0)
+        quantize_and_multiply("a", chunks[-1], xa_before)
+        rounded_middle = round_result(middle_tile, 0, T_TILE, SCALAR_COLUMNS_MIDDLE)
+        quantize_result(first_tile, 0, T_TILE, rounded_first)
+        store_words(first_tile)
+        quantize_result(middle_tile, 0, T_TILE, rounded_middle)
+        store_words(middle_tile)
 
-        last = TILES - 1
-        for r in range(PACK - 1):
-            add_bias_scalar(last, r)
-            store_y(last, r, r + 1)
-        add_bias_vector(last, PACK - 1)
-        store_y(last, PACK - 1, PACK)
+        for r in range(last_bank):
+            add_bias_on_scalar(last_tile, r)
+            store_result(last_tile, r, r + 1)
+        add_bias_on_vector(last_tile, last_bank)
+        store_result(last_tile, last_bank, PACK)
         half = T_TILE // 2
-        rounded_halves = [round_y(last, 0, half, 0, "y_half"), round_y(last, half, half, SCALAR_COLUMNS_LAST, "y_half")]
-        for h in range(2):
-            quantize_y(last, h * half, rounded_halves[h])
-        store_words(last)
+        rounded_left = round_result(last_tile, 0, half, 0)
+        rounded_right = round_result(last_tile, half, half, SCALAR_COLUMNS_LAST)
+        quantize_result(last_tile, 0, half, rounded_left)
+        quantize_result(last_tile, half, half, rounded_right)
+        store_words(last_tile)
         for q in range(P // QUADRANT):
             queue = nc.scalar if q % 2 == 0 else nc.sync
             queue.dma_start(
-                out=out_scales[4 * q : 4 * q + 4, :], in_=y_scales[QUADRANT * q : QUADRANT * q + 4, :].bitcast(I32)
+                out=out_scales[SCALE_ROWS * q : SCALE_ROWS * (q + 1), :],
+                in_=y_scales[QUADRANT * q : QUADRANT * q + SCALE_ROWS, :].bitcast(I32),
             )

from contextlib import ExitStack

import concourse.mybir as mybir

K, M, T = 1536, 512, 1536
FLOPS = 2 * 2 * K * M * T

F32 = mybir.dt.float32
BF16 = mybir.dt.bfloat16
I32 = mybir.dt.int32
U32 = mybir.dt.uint32
U16 = mybir.dt.uint16
U8 = mybir.dt.uint8
FP8X4 = mybir.dt.float8_e4m3fn_x4
FP4X4 = mybir.dt.float4_e2m1fn_x4
ALU = mybir.AluOpType
ACT = mybir.ActivationFunctionType

P = 128
PACK = 4
PASSES = K // (P * PACK)
T_TILE = 512
TILES = T // T_TILE
QUADRANT = 32
SCALE_ROWS = 4
W8_FIRST = 4
RUN = 4
SCALAR_COLUMNS_MIDDLE = 256
SCALAR_COLUMNS_LAST = 160


def interleaved(dst, src):
    return (
        dst.rearrange("p (c i j) -> p c j i", i=RUN, j=PACK),
        src.rearrange("p j (c i) -> p c j i", i=RUN),
    )


def tile_mix_feat_fm_crelupl_bias_kernel(
    tc, x, w4_words, w4_scales, w8_words, w8_scales, b, out_0, out_1, out_2
):
    nc = tc.nc
    x_rows = x.rearrange("(a p j) t -> a p j t", p=P, j=PACK)
    out_rows = out_0.rearrange("(p r) t -> p r t", r=PACK)
    out_words = out_1[0].rearrange("p t i -> p (t i)").bitcast(I32)
    out_scales = out_2[0].bitcast(I32)
    chunks = [(tile, a) for tile in range(TILES) for a in range(PASSES)]
    first_tile, middle_tile, last_tile = range(TILES)

    with ExitStack() as ctx:
        keep = ctx.enter_context(tc.tile_pool(name="keep", bufs=1))
        stage = ctx.enter_context(tc.tile_pool(name="stage", bufs=2))
        psum = ctx.enter_context(tc.psum_pool(name="psum", bufs=2))
        ctx.enter_context(tc.manual_schedule())

        planes_raw = keep.tile([P, PASSES, M], U8, align_bytes=64)
        planes = keep.tile([P, PACK, PASSES, P], U8, align_bytes=64)
        w4_raw = keep.tile([P, PASSES, 2 * M], U8, align_bytes=64)
        w4 = keep.tile([P, PACK, PASSES, 2 * P], U8, align_bytes=64)
        w8_raw = keep.tile([P, PASSES, M], I32, align_bytes=64)
        w8 = keep.tile([P, PACK, PASSES, P], I32, align_bytes=64)
        bias = keep.tile([P, PACK], F32)

        nc.vector.memset(planes_raw[:].bitcast(I32), 0)
        warm_in = keep.tile([P, 1], F32)
        warm_out = keep.tile([P, 1], F32)
        nc.vector.memset(warm_in[:], 0.0)
        nc.scalar.activation(out=warm_out[:], in_=warm_in[:], func=ACT.Relu)

        def load_scale_rows(rows):
            for i in rows:
                for scales, first in ((w8_scales, W8_FIRST), (w4_scales, 0)):
                    nc.sync.dma_start(
                        out=planes_raw[first + i : P : QUADRANT, :, :].bitcast(I32),
                        in_=scales.rearrange("a (q i) n -> i q a n", i=SCALE_ROWS)[i].bitcast(I32),
                    )

        nc.sync.dma_start(out=w4_raw[:].bitcast(I32), in_=w4_words.rearrange("a p m -> p a m").bitcast(I32))
        load_scale_rows(range(SCALE_ROWS // 2))
        nc.sync.dma_start(out=w8_raw[:], in_=w8_words.rearrange("a p n i -> p a (n i)").bitcast(I32))
        load_scale_rows(range(SCALE_ROWS // 2, SCALE_ROWS))
        raws = {}
        for tile, a in chunks:
            raw = keep.tile([P, PACK, T_TILE], F32, name="raw%d%d" % (tile, a))
            nc.sync.dma_start(out=raw[:], in_=x_rows[a, :, :, tile * T_TILE : (tile + 1) * T_TILE])
            raws[tile, a] = raw
            if (tile, a) == (middle_tile, 0):
                nc.sync.dma_start(out=bias[:], in_=b.rearrange("(p r) -> p r", r=PACK))

        nc.vector.tensor_copy(
            out=w4[:].bitcast(U16).rearrange("p r a m -> p r (a m)"),
            in_=w4_raw[:].bitcast(U16).rearrange("p a (m r) -> p r (a m)", r=PACK),
        )
        nc.vector.tensor_copy(
            out=w8[:].rearrange("p r a (c i) -> p (a c) r i", i=RUN),
            in_=w8_raw[:].rearrange("p a (c i r) -> p (a c) r i", i=RUN, r=PACK),
        )
        nc.vector.tensor_copy(
            out=planes[:].rearrange("p r a m -> p r (a m)"),
            in_=planes_raw[:].rearrange("p a (m r) -> p r (a m)", r=PACK),
        )

        def positive_part(chunk):
            xa = stage.tile([P, PACK * T_TILE], BF16, name="xa", bufs=3, align_bytes=64)
            dst, src = interleaved(xa[:], raws[chunk][:])
            nc.scalar.activation(out=dst, in_=src, func=ACT.Relu)
            return xa

        def negative_part(chunk):
            xb = stage.tile([P, PACK * T_TILE], BF16, name="xb", align_bytes=64)
            dst, src = interleaved(xb[:], raws[chunk][:])
            nc.vector.tensor_scalar(out=dst, in0=src, scalar1=-1.0, scalar2=0.0, op0=ALU.mult, op1=ALU.max)
            return xb

        banks = {}

        def quantize_and_multiply(feature, chunk, part):
            tile, a = chunk
            label = "%s%d%d" % (feature, tile, a)
            words = keep.tile([P, T_TILE], U32, name="words_" + label, align_bytes=64)
            scales = keep.tile([P, T_TILE], U8, name="scales_" + label, align_bytes=64)
            nc.vector.quantize_mx(out=words[:].bitcast(FP8X4), scales=scales[:], in_=part[:])
            opens = feature == "b" and a == 0
            closes = feature == "a" and a == PASSES - 1
            for r in range(PACK):
                if opens:
                    banks[tile, r] = psum.tile([P, T_TILE], F32, name="acc%d" % r)
                if feature == "a":
                    weights, weight_scales = w4[:, r, a, :].bitcast(FP4X4), planes[:, r, a, :]
                else:
                    weights, weight_scales = w8[:, r, a, :].bitcast(FP8X4), planes[W8_FIRST:P, r, a, :]
                nc.tensor.matmul_mx(
                    out=banks[tile, r][:],
                    lhsT=weights,
                    lhsT_scale=weight_scales,
                    rhs=words[:].bitcast(FP8X4),
                    rhs_scale=scales[:],
                    start=opens,
                    stop=closes,
                )

        results = [keep.tile([P, PACK, T_TILE], F32, name="y%d" % tile) for tile in range(TILES)]
        y_words = keep.tile([P, T], U32, align_bytes=64)
        y_scales = keep.tile([P, T], U8, align_bytes=64)

        def add_bias_on_scalar(tile, r):
            nc.scalar.activation(
                out=results[tile][:, r, :], in_=banks[tile, r][:], func=ACT.Identity, bias=bias[:, r : r + 1]
            )

        def add_bias_on_vector(tile, r):
            nc.vector.tensor_scalar(
                out=results[tile][:, r, :], in0=banks[tile, r][:], scalar1=bias[:, r : r + 1], scalar2=None, op0=ALU.add
            )

        def store_result(tile, r0, r1):
            cols = slice(tile * T_TILE, (tile + 1) * T_TILE)
            nc.sync.dma_start(out=out_rows[:, r0:r1, cols], in_=results[tile][:, r0:r1, :])

        def round_result(tile, c0, width, scalar_columns):
            rounded = keep.tile([P, PACK * width], BF16, name="rounded%d_%d" % (tile, c0), align_bytes=64)
            dst, src = interleaved(rounded[:], results[tile][:, :, c0 : c0 + width])
            split = (width - scalar_columns) // RUN
            nc.vector.tensor_copy(out=dst[:, :split], in_=src[:, :split])
            if scalar_columns > 0:
                nc.scalar.copy(out=dst[:, split:], in_=src[:, split:])
            return rounded

        def quantize_result(tile, c0, width, rounded):
            cols = slice(tile * T_TILE + c0, tile * T_TILE + c0 + width)
            nc.vector.quantize_mx(out=y_words[:, cols].bitcast(FP8X4), scales=y_scales[:, cols], in_=rounded[:])

        def store_words(tile):
            cols = slice(tile * T_TILE, (tile + 1) * T_TILE)
            nc.sync.dma_start(out=out_words[:, cols], in_=y_words[:, cols].bitcast(I32))

        last_bank = PACK - 1
        xa_before = None
        for step, chunk in enumerate(chunks):
            xa = positive_part(chunk)
            xb = negative_part(chunk)
            if step > 0:
                quantize_and_multiply("a", chunks[step - 1], xa_before)
            quantize_and_multiply("b", chunk, xb)
            xa_before = xa
            if chunk == (middle_tile, 1):
                for r in range(last_bank):
                    add_bias_on_scalar(first_tile, r)
                add_bias_on_vector(first_tile, last_bank)
                store_result(first_tile, 0, PACK)
            if chunk == (last_tile, 1):
                add_bias_on_vector(middle_tile, last_bank)

        for r in range(last_bank):
            add_bias_on_scalar(middle_tile, r)
        store_result(middle_tile, 0, PACK)
        rounded_first = round_result(first_tile, 0, T_TILE, 0)
        quantize_and_multiply("a", chunks[-1], xa_before)
        rounded_middle = round_result(middle_tile, 0, T_TILE, SCALAR_COLUMNS_MIDDLE)
        quantize_result(first_tile, 0, T_TILE, rounded_first)
        store_words(first_tile)
        quantize_result(middle_tile, 0, T_TILE, rounded_middle)
        store_words(middle_tile)

        for r in range(last_bank):
            add_bias_on_scalar(last_tile, r)
            store_result(last_tile, r, r + 1)
        add_bias_on_vector(last_tile, last_bank)
        store_result(last_tile, last_bank, PACK)
        half = T_TILE // 2
        rounded_left = round_result(last_tile, 0, half, 0)
        rounded_right = round_result(last_tile, half, half, SCALAR_COLUMNS_LAST)
        quantize_result(last_tile, 0, half, rounded_left)
        quantize_result(last_tile, half, half, rounded_right)
        store_words(last_tile)
        for q in range(P // QUADRANT):
            queue = nc.scalar if q % 2 == 0 else nc.sync
            queue.dma_start(
                out=out_scales[SCALE_ROWS * q : SCALE_ROWS * (q + 1), :],
                in_=y_scales[QUADRANT * q : QUADRANT * q + SCALE_ROWS, :].bitcast(I32),
            )
